import numpy as np
import ml_dtypes


def mxq(x, axis, fmt="e4m3"):
    dtype, down = {"e4m3": (ml_dtypes.float8_e4m3fn, 7), "e5m2": (ml_dtypes.float8_e5m2, 14)}[fmt]
    v = np.moveaxis(np.asarray(x, np.float32).astype(ml_dtypes.bfloat16).astype(np.float64), axis, -1)
    blocks = v.reshape(v.shape[:-1] + (-1, 32))
    amax = np.abs(blocks).max(-1, keepdims=True)
    byte = np.maximum(np.where(amax > 0, np.frexp(amax)[1] - 1 + 127, 0) - down, 1)
    scale = np.exp2(byte - 127.0)
    codes = (blocks / scale).astype(np.float32).astype(dtype).astype(np.float64)
    return np.moveaxis((codes * scale).reshape(v.shape), -1, axis)


WIDE = False


def mx_kscale(k):
    if not WIDE:
        return np.ones(k)
    levels = np.array([10, -10, 5, -5, 0])
    if k % 512:
        return np.exp2(np.random.permutation(np.resize(levels, k // 32))).repeat(32)
    a = np.empty((k // 512, 16))
    for p in range(k // 512):
        a[p, :8] = np.random.permutation(np.resize(levels, 8))
        for g in range(8):
            far = levels[np.abs(levels - a[p, g]) >= 10]
            a[p, g + 8] = far[np.random.randint(len(far))]
    return np.exp2(a.ravel()).repeat(32)


def f64(x):
    return np.asarray(x).astype(np.float64)


def striped(idx):
    return np.tile(idx.reshape(-1, 16).T, (8, 1)).astype(np.uint16)


def unstriped(offs):
    return offs[:16].T.reshape(-1).astype(np.int64)


def striped8(idx):
    return np.concatenate([x.reshape(-1, 16).T for x in idx]).astype(np.uint16)


def runs(offs, k):
    lists = np.stack([offs[16 * r : 16 * r + 16].T.reshape(-1) for r in range(8)]).astype(np.int64)
    return lists[np.arange(k) % 512 // 64]


def pack_weight(w):
    k, n = w.shape
    w = f64(np.asarray(w, np.float32).astype(ml_dtypes.bfloat16)).reshape(k // 32, 32, n)
    amax = np.abs(w).max(1)
    byte = np.clip(np.where(amax > 0, np.frexp(amax)[1] - 1 + 127 - 7, 1), 1, 254)
    scaled = (w * np.exp2(127.0 - byte)[:, None, :]).reshape(k, n).astype(np.float32)
    words = np.ascontiguousarray(scaled.reshape(k // 512, 128, 4, n).transpose(0, 1, 3, 2)).astype(ml_dtypes.float8_e4m3fn).view(np.uint8)
    return words, np.ascontiguousarray(byte.astype(np.uint8).reshape(k // 512, 16, n))


def unpack_weight(words, scales):
    g, p, n, _ = words.shape
    vals = np.ascontiguousarray(words).view(ml_dtypes.float8_e4m3fn).astype(np.float64) * np.repeat(np.exp2(scales.astype(np.float64) - 127.0), 8, axis=1)[..., None]
    return vals.transpose(0, 1, 3, 2).reshape(g * 512, n)

def planes(y):
    n, m = y.shape
    v = y.astype(np.float32).astype(ml_dtypes.bfloat16).astype(np.float64).reshape(n // 32, 32, m)
    top = np.abs(v).max(1)
    byte = np.clip(np.where(top > 0, np.frexp(top)[1] - 1 + 127 - 7, 1), 1, 254)
    codes = (v * np.exp2(127.0 - byte)[:, None, :]).reshape(n, m).astype(np.float32).astype(ml_dtypes.float8_e4m3fn).view(np.uint8)
    words = codes.reshape(n // 512, 128, 4, m).transpose(0, 1, 3, 2)
    return np.ascontiguousarray(words), np.ascontiguousarray(byte.astype(np.uint8).reshape(n // 512, 16, m))


K, T, S, N, H, G, W, J = 512, 1024, 512, 512, 512, 2048, 256, 512


def setup_inputs():
    n = np.random.standard_normal
    s = mx_kscale(K)[:, None]
    u = mx_kscale(S)
    packed_xT = pack_weight(n((K, T)) * s)
    packed_w1 = pack_weight(n((K, H)) / np.sqrt(K) / s)
    packed_dT = pack_weight(n((K, G)) / s)
    packed_w2 = pack_weight(n((H, N)) / np.sqrt(2 * H) / u[:, None])
    packed_w3 = pack_weight(n((H, N)) / np.sqrt(2 * H) / u[:, None])
    perm = np.stack([np.random.permutation(S) for _ in range(8)])
    return {
        "x_words": packed_xT[0],
        "x_scales": packed_xT[1],
        "w1_words": packed_w1[0],
        "w1_scales": packed_w1[1],
        "d_words": packed_dT[0],
        "d_scales": packed_dT[1],
        "tab": n((H, J)).astype(np.float32),
        "gn": (np.random.uniform(0.5, 1.5, (H, 1)) * u[:, None]).astype(np.float32),
        "gk": (np.random.uniform(0.5, 1.5, (H, 1)) * u[:, None]).astype(np.float32),
        "w2_words": packed_w2[0],
        "w2_scales": packed_w2[1],
        "w3_words": packed_w3[0],
        "w3_scales": packed_w3[1],
        "offs": striped(np.random.permutation(T)[:S]),
        "kidx": striped8(np.random.randint(0, G, (8, H))),
        "two": striped(np.random.permutation(T)[:S]),
        "n1": striped8(perm[:, :W]),
        "n2": striped8(perm[:, W:]),
        "n3": striped8(np.random.randint(0, J, (8, S))),
        "n4": striped8(np.random.randint(0, J, (8, S))),
        "n5": striped8(np.stack([np.random.permutation(S) for _ in range(8)])),
        "n6": striped(np.random.permutation(S)),
    }


def reference(x_words, x_scales, w1_words, w1_scales, d_words, d_scales, tab, gn, gk, w2_words, w2_scales, w3_words, w3_scales, offs, kidx, two, n1, n2, n3, n4, n5, n6):
    xq = unpack_weight(x_words, x_scales)[:, unstriped(offs)]
    y = unpack_weight(w1_words, w1_scales).T @ xq
    pa = y[np.arange(H)[:, None], runs(n1, H)]
    pb = y[np.arange(H)[:, None], runs(n2, H)]
    rb = pa * pb
    ra = pa + pb
    ds = np.zeros((H, S))
    ds[np.arange(H)[:, None], runs(n1, H)] = ra
    dt = ds.copy()
    dt[np.arange(H)[:, None], runs(n2, H)] = rb
    z = f64(gn) * dt
    d_kidx = unpack_weight(d_words, d_scales)[np.arange(K)[:, None], runs(kidx, K)]
    x_two = unpack_weight(x_words, x_scales)[:, unstriped(two)]
    s = 0.0625 * (d_kidx.T @ x_two)
    z2 = f64(gk) * ((s[np.arange(H)[:, None], runs(n5, H)]) * (f64(tab)[np.arange(H)[:, None], runs(n3, H)]) + f64(tab)[np.arange(H)[:, None], runs(n4, H)])
    h = unpack_weight(w2_words, w2_scales).T @ mxq(z, 0, "e4m3") + unpack_weight(w3_words, w3_scales).T @ mxq(z2, 0, "e4m3")
    pa2 = h[:, unstriped(n6)]
    out_0 = (2.0 * (h * pa2)) / ((h) ** 2 + (pa2) ** 2 + 0.5)
    return (out_0,) + planes(out_0)

@@ -1,0 +1,262 @@
+from contextlib import ExitStack
+
+import concourse.mybir as mybir
+
+F32 = mybir.dt.float32
+BF16 = mybir.dt.bfloat16
+I32 = mybir.dt.int32
+U32 = mybir.dt.uint32
+U16 = mybir.dt.uint16
+U8 = mybir.dt.uint8
+FP8X4 = mybir.dt.float8_e4m3fn_x4
+ACT = mybir.ActivationFunctionType
+ALU = mybir.AluOpType
+
+P = 128
+PACK = 4
+S = 512
+T = 1024
+G = 2048
+PAIRS = 256
+FLOPS = 4 * 2 * 512 * 512 * 512
+Z2_CHUNKS = ((0, 256), (256, 256))
+OUT_CHUNKS = ((0, 128), (128, 256), (384, 128))
+
+
+def words_view(words):
+    return words[0].rearrange("p n t -> p (n t)").bitcast(I32)
+
+
+def load_scale_rows(queue, plane, scales, first):
+    for q in range(4):
+        queue.dma_start(out=plane[32 * q + first : 32 * q + first + 4, :].bitcast(I32), in_=scales[0, 4 * q : 4 * q + 4, :].bitcast(I32))
+
+
+def deal_views(dealt, plain, run):
+    return (
+        dealt.rearrange("p (t b i) -> p b t i", t=PACK, i=run),
+        plain.rearrange("p (b i t) -> p b t i", t=PACK, i=run),
+    )
+
+
+def weave_out(woven):
+    return woven.rearrange("p (c i t) -> p c t i", t=PACK, i=4)
+
+
+def weave_in(planes):
+    return planes.rearrange("p t (c i) -> p c t i", i=4)
+
+
+def entries(offsets, start, count):
+    return offsets[:, start // 16 : (start + count) // 16]
+
+
+def tile_picked_jkeybondkindaharm_none_po_kernel(
+    tc, x_words, x_scales, w1_words, w1_scales, d_words, d_scales, tab, gn, gk, w2_words, w2_scales, w3_words, w3_scales,
+    offs, kidx, two, n1, n2, n3, n4, n5, n6, out_0, out_1, out_2,
+):
+    nc = tc.nc
+    with ExitStack() as ctx:
+        lists = ctx.enter_context(tc.tile_pool(name="lists", bufs=1))
+        sb = ctx.enter_context(tc.tile_pool(name="sb", bufs=1))
+        psum = ctx.enter_context(tc.psum_pool(name="psum", bufs=1))
+
+        def tile(name, shape, dtype, tag=None):
+            return sb.tile(shape, dtype, name=name, tag=tag or name, align_bytes=64)
+
+        def load_list(name, source):
+            offsets = lists.tile(list(source.shape), U16, name=name)
+            nc.sync.dma_start(offsets[:], source)
+            return offsets
+
+        xw = tile("xw", [P, T], U32)
+        xs = tile("xs", [P, T], U8)
+        dw = tile("dw", [P, G], U32)
+        ds = tile("ds", [P, G], U8)
+        w1w = tile("w1w", [P, S], U32)
+        w1s = tile("w1s", [P, S], U8)
+        w23s = tile("w23s", [P, S], U8)
+        key_scales = tile("key_scales", [P, S], U8)
+        quarter = tile("quarter", [P, 1], F32)
+        for plane in (xs, w1s, ds, key_scales, w23s):
+            nc.vector.memset(plane[:].bitcast(I32), 0)
+        nc.vector.memset(quarter[:], 0.25)
+
+        tab_rows = tab.rearrange("(p t) j -> p t j", t=PACK)
+        tab_raw = [tile("tab_raw0", [P, 2, S], F32)]
+        gk_sb = tile("gk_sb", [P, PACK], F32)
+
+        offs_l = load_list("offs_l", offs)
+        nc.sync.dma_start(out=xw[:].bitcast(I32), in_=words_view(x_words))
+        two_l = load_list("two_l", two)
+        nc.sync.dma_start(out=w1w[:].bitcast(I32), in_=words_view(w1_words))
+        nc.sync.dma_start(out=gk_sb[:], in_=gk.rearrange("(p t) o -> p (t o)", t=PACK))
+        nc.sync.dma_start(out=tab_raw[0][:], in_=tab_rows[:, 0:2, :])
+        load_scale_rows(nc.sync, xs, x_scales, 0)
+        load_scale_rows(nc.sync, w1s, w1_scales, 0)
+        n3_l = load_list("n3_l", n3)
+        n4_l = load_list("n4_l", n4)
+        kidx_l = load_list("kidx_l", kidx)
+        n1_l = load_list("n1_l", n1)
+        n2_l = load_list("n2_l", n2)
+        n5_l = load_list("n5_l", n5)
+        n6_l = load_list("n6_l", n6)
+        nc.sync.dma_start(out=dw[:].bitcast(I32), in_=words_view(d_words))
+        load_scale_rows(nc.sync, ds, d_scales, 14)
+        load_scale_rows(nc.sync, w23s, w2_scales, 0)
+        load_scale_rows(nc.sync, w23s, w3_scales, 4)
+
+        xa_w = tile("xa_w", [P, S], U32)
+        xa_s = tile("xa_s", [P, S], U8)
+        nc.vector.tensor_copy(out=xa_w[:], in_=xw[:].indirect(offs_l[:]))
+        xb_w = tile("xb_w", [P, S], U32)
+        nc.vector.tensor_copy(out=xb_w[:], in_=xw[:].indirect(two_l[:]))
+        nc.vector.tensor_copy(out=xa_s[:], in_=xs[:].indirect(offs_l[:]))
+        w1w_d = tile("w1w_d", [P, S], U32)
+        w1s_d = tile("w1s_d", [P, S], U8)
+        nc.scalar.copy(*deal_views(w1w_d[:], w1w[:], 4))
+        nc.vector.tensor_copy(*deal_views(w1s_d[:], w1s[:], 16))
+        tab_raw.append(tile("tab_raw1", [P, 2, S], F32, "w1w"))
+        nc.sync.dma_start(out=tab_raw[1][:], in_=tab_rows[:, 2:4, :])
+        y_ps = [psum.tile([P, S], F32, name="y_ps%d" % t, tag="bank%d" % t) for t in range(PACK)]
+        for t in range(PACK):
+            cols = slice(P * t, P * (t + 1))
+            nc.tensor.matmul_mx(out=y_ps[t][:], lhsT=w1w_d[:, cols].bitcast(FP8X4), lhsT_scale=w1s_d[:, cols],
+                                rhs=xa_w[:].bitcast(FP8X4), rhs_scale=xa_s[:], start=True, stop=True)
+
+        xb_s = tile("xb_s", [P, S], U8)
+        kw_g = tile("kw_g", [P, S], U32, "w1s")
+        kw_d = tile("kw_d", [P, S], U32)
+        nc.vector.tensor_copy(out=kw_g[:], in_=dw[:].indirect(kidx_l[:]))
+        nc.vector.tensor_copy(out=xb_s[:], in_=xs[:].indirect(two_l[:]))
+        nc.vector.tensor_copy(*deal_views(kw_d[:].bitcast(I32), kw_g[:].bitcast(I32), 4))
+        ks_g = tile("ks_g", [P, S], U8, "w1s")
+        ks_d = tile("ks_d", [P, S], U8)
+        nc.vector.tensor_copy(out=ks_g[:], in_=ds[:].indirect(kidx_l[:]))
+        nc.vector.tensor_copy(*deal_views(ks_d[:], ks_g[:], 16))
+        for q in range(4):
+            nc.sync.dma_start(out=key_scales[32 * q : 32 * q + 4, :].bitcast(I32), in_=ks_d[32 * q + 14 : 32 * q + 18, :].bitcast(I32))
+        gn_sb = tile("gn_sb", [P, PACK], F32, "xs")
+        nc.sync.dma_start(out=gn_sb[:], in_=gn.rearrange("(p t) o -> p (t o)", t=PACK))
+        s_ps = [psum.tile([P, S], F32, name="s_ps%d" % t, tag="bank%d" % (PACK + t)) for t in range(PACK)]
+        for t in range(PACK):
+            cols = slice(P * t, P * (t + 1))
+            nc.tensor.matmul_mx(out=s_ps[t][:], lhsT=kw_d[:, cols].bitcast(FP8X4), lhsT_scale=key_scales[:, cols],
+                                rhs=xb_w[:].bitcast(FP8X4), rhs_scale=xb_s[:], start=True, stop=True)
+
+        z_planes = tile("z_planes", [P, PACK, S], BF16)
+        dts = []
+        for t in range(PACK):
+            y_sb = tile("y_sb%d" % t, [P, S], F32)
+            pa = tile("pa%d" % t, [P, PAIRS], F32)
+            pb = tile("pb%d" % t, [P, PAIRS], F32)
+            dt_sb = tile("dt_sb%d" % t, [P, S], F32, "w1s" if t == 0 else None)
+            nc.scalar.copy(out=y_sb[:], in_=y_ps[t][:])
+            nc.scalar.activation(out=pa[:], in_=y_sb[:].indirect(n1_l[:]), func=ACT.Copy)
+            nc.scalar.activation(out=pb[:], in_=y_sb[:].indirect(n2_l[:]), func=ACT.Copy)
+            nc.vector.tensor_tensor(out=dt_sb[:].indirect(n1_l[:]), in0=pa[:], in1=pb[:], op=ALU.add)
+            nc.vector.tensor_tensor(out=dt_sb[:].indirect(n2_l[:]), in0=pa[:], in1=pb[:], op=ALU.mult)
+            dts.append(dt_sb)
+
+        tab_g = [tile("tab_g%d" % t, [P, S], F32) for t in range(PACK)]
+        s_sb = [tile("s_sb%d" % t, [P, S], F32) for t in range(PACK)]
+        for t in range(PACK):
+            nc.scalar.activation(out=s_sb[t][:], in_=s_ps[t][:], func=ACT.Copy, scale=0.0625)
+        for t in range(PACK):
+            nc.scalar.activation(out=tab_g[t][:], in_=tab_raw[t // 2][:, t % 2, :], func=ACT.Copy, scale=gk_sb[:, t : t + 1])
+
+        w2w = tile("w2w", [P, S], U32, "tab_raw0")
+        w3w = tile("w3w", [P, S], U32, "xw")
+        nc.sync.dma_start(out=w2w[:].bitcast(I32), in_=words_view(w2_words))
+        nc.sync.dma_start(out=w3w[:].bitcast(I32), in_=words_view(w3_words))
+        z2_w = tile("z2_w", [P, S], U32)
+        z2_s = tile("z2_s", [P, S], U8)
+        z_w = tile("z_w", [P, S], U32)
+        z_s = tile("z_s", [P, S], U8)
+
+        def z2_chunk(c):
+            start, width = Z2_CHUNKS[c]
+            s5 = tile("s5_%d" % c, [P, PACK, width], F32)
+            t3 = tile("t3_%d" % c, [P, PACK, width], F32, "y_sb0" if c == 1 else None)
+            t4 = tile("t4_%d" % c, [P, PACK, width], F32, "s_sb3" if c == 1 else None)
+            prod = tile("prod_%d" % c, [P, PACK, width], F32)
+            woven = tile("z2_woven%d" % c, [P, PACK * width], BF16)
+            for t in range(PACK):
+                nc.scalar.activation(out=s5[:, t, :], in_=s_sb[t][:].indirect(entries(n5_l, start, width)), func=ACT.Copy)
+            for t in range(PACK):
+                nc.scalar.activation(out=t3[:, t, :], in_=tab_g[t][:].indirect(entries(n3_l, start, width)), func=ACT.Copy)
+            for t in range(PACK):
+                nc.scalar.activation(out=t4[:, t, :], in_=tab_g[t][:].indirect(entries(n4_l, start, width)), func=ACT.Copy)
+            nc.vector.tensor_tensor(out=prod[:], in0=s5[:], in1=t3[:], op=ALU.mult)
+            nc.vector.tensor_tensor(out=weave_out(woven[:]), in0=weave_in(prod[:]), in1=weave_in(t4[:]), op=ALU.add)
+            nc.vector.quantize_mx(out=z2_w[:, start : start + width].bitcast(FP8X4), scales=z2_s[:, start : start + width], in_=woven[:])
+
+        z2_chunk(0)
+        for t in range(PACK):
+            nc.vector.tensor_scalar(out=z_planes[:, t, :], in0=dts[t][:], scalar1=gn_sb[:, t : t + 1], scalar2=None, op0=ALU.mult)
+        z_woven = tile("z_woven", [P, PACK * S], BF16)
+        nc.vector.tensor_copy(out=weave_out(z_woven[:]), in_=weave_in(z_planes[:]))
+        w23s_d = tile("w23s_d", [P, S], U8)
+        nc.vector.tensor_copy(*deal_views(w23s_d[:], w23s[:], 16))
+        nc.vector.quantize_mx(out=z_w[:].bitcast(FP8X4), scales=z_s[:], in_=z_woven[:])
+        z2_chunk(1)
+
+        w2w_d = tile("w2w_d", [P, S], U32)
+        w3w_d = tile("w3w_d", [P, S], U32)
+        nc.scalar.copy(*deal_views(w2w_d[:], w2w[:], 4))
+        nc.scalar.copy(*deal_views(w3w_d[:], w3w[:], 4))
+
+        h_ps = [psum.tile([P, S], F32, name="h_ps%d" % t, tag="bank%d" % t) for t in range(PACK)]
+        for t in range(PACK):
+            cols = slice(P * t, P * (t + 1))
+            nc.tensor.matmul_mx(out=h_ps[t][:], lhsT=w2w_d[:, cols].bitcast(FP8X4), lhsT_scale=w23s_d[:, cols],
+                                rhs=z_w[:].bitcast(FP8X4), rhs_scale=z_s[:], start=True, stop=False)
+        for c, (start, width) in enumerate(Z2_CHUNKS):
+            span = slice(start, start + width)
+            for t in range(PACK):
+                cols = slice(P * t, P * (t + 1))
+                nc.tensor.matmul_mx(out=h_ps[t][:, span], lhsT=w3w_d[:, cols].bitcast(FP8X4), lhsT_scale=w23s_d[4:P, cols],
+                                    rhs=z2_w[:, span].bitcast(FP8X4), rhs_scale=z2_s[:, span], start=False, stop=(c == len(Z2_CHUNKS) - 1))
+
+        h_sb = tile("h_sb", [P, PACK, S], F32)
+        for t in range(PACK):
+            if t % 2:
+                nc.scalar.copy(out=h_sb[:, t, :], in_=h_ps[t][:])
+            else:
+                nc.vector.tensor_copy(out=h_sb[:, t, :], in_=h_ps[t][:])
+
+        out_w = tile("out_w", [P, S], U32)
+        out_s = tile("out_s", [P, S], U8)
+        out_rows = out_0.rearrange("(p t) j -> p t j", t=PACK)
+        out_words = words_view(out_1)
+        for c, (start, width) in enumerate(OUT_CHUNKS):
+            span = slice(start, start + width)
+            shape = [P, PACK, width]
+            other = tile("other%d" % c, shape, F32)
+            other_sq = tile("other_sq%d" % c, shape, F32)
+            num = tile("num%d" % c, shape, F32)
+            squares = tile("squares%d" % c, shape, F32)
+            root = tile("root%d" % c, shape, F32)
+            inverse = tile("inverse%d" % c, shape, F32)
+            result = tile("result%d" % c, shape, F32)
+            woven = tile("out_woven%d" % c, [P, PACK * width], BF16)
+            h_sq = tile("h_sq%d" % c, shape, F32)
+            for t in range(PACK):
+                if t % 2:
+                    nc.scalar.activation(out=other[:, t, :], in_=h_sb[:, t, :].indirect(entries(n6_l, start, width)), func=ACT.Copy)
+                else:
+                    nc.vector.tensor_copy(out=other[:, t, :], in_=h_sb[:, t, :].indirect(entries(n6_l, start, width)))
+            nc.scalar.activation(out=h_sq[:], in_=h_sb[:, :, span], func=ACT.Square)
+            nc.scalar.activation(out=other_sq[:], in_=other[:], func=ACT.Square)
+            nc.vector.tensor_tensor(out=num[:], in0=other[:], in1=h_sb[:, :, span], op=ALU.mult)
+            nc.vector.tensor_tensor(out=squares[:], in0=other_sq[:], in1=h_sq[:], op=ALU.add)
+            nc.scalar.activation(out=root[:], in_=squares[:], func=ACT.Abs_reciprocal_sqrt, scale=0.5, bias=quarter[:])
+            nc.scalar.activation(out=inverse[:], in_=root[:], func=ACT.Square)
+            nc.vector.tensor_tensor(out=result[:], in0=num[:], in1=inverse[:], op=ALU.mult)
+            nc.sync.dma_start(out=out_rows[:, :, span], in_=result[:])
+            nc.vector.tensor_copy(out=weave_out(woven[:]), in_=weave_in(result[:]))
+            nc.vector.quantize_mx(out=out_w[:, span].bitcast(FP8X4), scales=out_s[:, span], in_=woven[:])
+            nc.sync.dma_start(out=out_words[:, span], in_=out_w[:, span].bitcast(I32))
+        for q in range(4):
+            queue = nc.scalar if q % 2 else nc.sync
+            queue.dma_start(out=out_2[0, 4 * q : 4 * q + 4, :].bitcast(I32), in_=out_s[32 * q : 32 * q + 4, :].bitcast(I32))

@@ -20,7 +20,7 @@ G = 2048
 PAIRS = 256
 FLOPS = 4 * 2 * 512 * 512 * 512
 Z2_CHUNKS = ((0, 256), (256, 256))
-OUT_CHUNKS = ((0, 128), (128, 256), (384, 128))
+OUT_CHUNKS = ((0, 256), (256, 256))
 
 
 def words_view(words):
@@ -59,10 +59,14 @@ def tile_picked_jkeybondkindaharm_none_po_kernel(
     with ExitStack() as ctx:
         lists = ctx.enter_context(tc.tile_pool(name="lists", bufs=1))
         sb = ctx.enter_context(tc.tile_pool(name="sb", bufs=1))
+        turn = ctx.enter_context(tc.tile_pool(name="turn", bufs=1))
         psum = ctx.enter_context(tc.psum_pool(name="psum", bufs=1))
 
         def tile(name, shape, dtype, tag=None):
             return sb.tile(shape, dtype, name=name, tag=tag or name, align_bytes=64)
+
+        def in_turn(name, shape, dtype, offset):
+            return turn.tile(shape, dtype, name=name, align_bytes=64, offset=offset)
 
         def load_list(name, source):
             offsets = lists.tile(list(source.shape), U16, name=name)
@@ -75,10 +79,10 @@ def tile_picked_jkeybondkindaharm_none_po_kernel(
         ds = tile("ds", [P, G], U8)
         w1w = tile("w1w", [P, S], U32)
         w1s = tile("w1s", [P, S], U8)
-        w23s = tile("w23s", [P, S], U8)
         key_scales = tile("key_scales", [P, S], U8)
         quarter = tile("quarter", [P, 1], F32)
-        for plane in (xs, w1s, ds, key_scales, w23s):
+        nc.gpsimd.memset(ds[:].bitcast(I32), 0)
+        for plane in (xs, w1s, key_scales):
             nc.vector.memset(plane[:].bitcast(I32), 0)
         nc.vector.memset(quarter[:], 0.25)
 
@@ -86,31 +90,27 @@ def tile_picked_jkeybondkindaharm_none_po_kernel(
         tab_raw = [tile("tab_raw0", [P, 2, S], F32)]
         gk_sb = tile("gk_sb", [P, PACK], F32)
 
+        load_scale_rows(nc.gpsimd, ds, d_scales, 14)
         offs_l = load_list("offs_l", offs)
         nc.sync.dma_start(out=xw[:].bitcast(I32), in_=words_view(x_words))
         two_l = load_list("two_l", two)
         nc.sync.dma_start(out=w1w[:].bitcast(I32), in_=words_view(w1_words))
-        nc.sync.dma_start(out=gk_sb[:], in_=gk.rearrange("(p t) o -> p (t o)", t=PACK))
         nc.sync.dma_start(out=tab_raw[0][:], in_=tab_rows[:, 0:2, :])
-        load_scale_rows(nc.sync, xs, x_scales, 0)
-        load_scale_rows(nc.sync, w1s, w1_scales, 0)
+        nc.sync.dma_start(out=gk_sb[:], in_=gk.rearrange("(p t) o -> p (t o)", t=PACK))
         n3_l = load_list("n3_l", n3)
         n4_l = load_list("n4_l", n4)
-        kidx_l = load_list("kidx_l", kidx)
+        load_scale_rows(nc.sync, xs, x_scales, 0)
+        load_scale_rows(nc.sync, w1s, w1_scales, 0)
         n1_l = load_list("n1_l", n1)
         n2_l = load_list("n2_l", n2)
+        kidx_l = load_list("kidx_l", kidx)
+        nc.sync.dma_start(out=dw[:].bitcast(I32), in_=words_view(d_words))
         n5_l = load_list("n5_l", n5)
         n6_l = load_list("n6_l", n6)
-        nc.sync.dma_start(out=dw[:].bitcast(I32), in_=words_view(d_words))
-        load_scale_rows(nc.sync, ds, d_scales, 14)
-        load_scale_rows(nc.sync, w23s, w2_scales, 0)
-        load_scale_rows(nc.sync, w23s, w3_scales, 4)
 
         xa_w = tile("xa_w", [P, S], U32)
         xa_s = tile("xa_s", [P, S], U8)
         nc.vector.tensor_copy(out=xa_w[:], in_=xw[:].indirect(offs_l[:]))
-        xb_w = tile("xb_w", [P, S], U32)
-        nc.vector.tensor_copy(out=xb_w[:], in_=xw[:].indirect(two_l[:]))
         nc.vector.tensor_copy(out=xa_s[:], in_=xs[:].indirect(offs_l[:]))
         w1w_d = tile("w1w_d", [P, S], U32)
         w1s_d = tile("w1s_d", [P, S], U8)
@@ -124,13 +124,11 @@ def tile_picked_jkeybondkindaharm_none_po_kernel(
             nc.tensor.matmul_mx(out=y_ps[t][:], lhsT=w1w_d[:, cols].bitcast(FP8X4), lhsT_scale=w1s_d[:, cols],
                                 rhs=xa_w[:].bitcast(FP8X4), rhs_scale=xa_s[:], start=True, stop=True)
 
+        xb_w = tile("xb_w", [P, S], U32)
+        nc.vector.tensor_copy(out=xb_w[:], in_=xw[:].indirect(two_l[:]))
         xb_s = tile("xb_s", [P, S], U8)
-        kw_g = tile("kw_g", [P, S], U32, "w1s")
-        kw_d = tile("kw_d", [P, S], U32)
-        nc.vector.tensor_copy(out=kw_g[:], in_=dw[:].indirect(kidx_l[:]))
         nc.vector.tensor_copy(out=xb_s[:], in_=xs[:].indirect(two_l[:]))
-        nc.vector.tensor_copy(*deal_views(kw_d[:].bitcast(I32), kw_g[:].bitcast(I32), 4))
-        ks_g = tile("ks_g", [P, S], U8, "w1s")
+        ks_g = in_turn("ks_g", [P, S], U8, 0)
         ks_d = tile("ks_d", [P, S], U8)
         nc.vector.tensor_copy(out=ks_g[:], in_=ds[:].indirect(kidx_l[:]))
         nc.vector.tensor_copy(*deal_views(ks_d[:], ks_g[:], 16))
@@ -138,25 +136,37 @@ def tile_picked_jkeybondkindaharm_none_po_kernel(
             nc.sync.dma_start(out=key_scales[32 * q : 32 * q + 4, :].bitcast(I32), in_=ks_d[32 * q + 14 : 32 * q + 18, :].bitcast(I32))
         gn_sb = tile("gn_sb", [P, PACK], F32, "xs")
         nc.sync.dma_start(out=gn_sb[:], in_=gn.rearrange("(p t) o -> p (t o)", t=PACK))
+        w23s = tile("w23s", [P, S], U8, "ds")
+        nc.gpsimd.memset(w23s[:].bitcast(I32), 0)
+        load_scale_rows(nc.sync, w23s, w2_scales, 0)
+        load_scale_rows(nc.sync, w23s, w3_scales, 4)
         s_ps = [psum.tile([P, S], F32, name="s_ps%d" % t, tag="bank%d" % (PACK + t)) for t in range(PACK)]
-        for t in range(PACK):
-            cols = slice(P * t, P * (t + 1))
-            nc.tensor.matmul_mx(out=s_ps[t][:], lhsT=kw_d[:, cols].bitcast(FP8X4), lhsT_scale=key_scales[:, cols],
-                                rhs=xb_w[:].bitcast(FP8X4), rhs_scale=xb_s[:], start=True, stop=True)
+
+        def scores():
+            for t in range(PACK):
+                cols = slice(P * t, P * (t + 1))
+                nc.tensor.matmul_mx(out=s_ps[t][:], lhsT=kw_d[:, cols].bitcast(FP8X4), lhsT_scale=key_scales[:, cols],
+                                    rhs=xb_w[:].bitcast(FP8X4), rhs_scale=xb_s[:], start=True, stop=True)
 
         z_planes = tile("z_planes", [P, PACK, S], BF16)
         dts = []
         for t in range(PACK):
             y_sb = tile("y_sb%d" % t, [P, S], F32)
-            pa = tile("pa%d" % t, [P, PAIRS], F32)
-            pb = tile("pb%d" % t, [P, PAIRS], F32)
-            dt_sb = tile("dt_sb%d" % t, [P, S], F32, "w1s" if t == 0 else None)
+            pa = in_turn("pa%d" % t, [P, PAIRS], F32, 2048 * (t + 2))
+            pb = in_turn("pb%d" % t, [P, PAIRS], F32, 2048 * (t + 2) + 1024)
+            dt_sb = in_turn("dt_sb%d" % t, [P, S], F32, 2048 * t)
             nc.scalar.copy(out=y_sb[:], in_=y_ps[t][:])
             nc.scalar.activation(out=pa[:], in_=y_sb[:].indirect(n1_l[:]), func=ACT.Copy)
             nc.scalar.activation(out=pb[:], in_=y_sb[:].indirect(n2_l[:]), func=ACT.Copy)
             nc.vector.tensor_tensor(out=dt_sb[:].indirect(n1_l[:]), in0=pa[:], in1=pb[:], op=ALU.add)
             nc.vector.tensor_tensor(out=dt_sb[:].indirect(n2_l[:]), in0=pa[:], in1=pb[:], op=ALU.mult)
             dts.append(dt_sb)
+            if t == 0:
+                kw_g = in_turn("kw_g", [P, S], U32, 3072)
+                kw_d = tile("kw_d", [P, S], U32)
+                nc.vector.tensor_copy(out=kw_g[:], in_=dw[:].indirect(kidx_l[:]))
+                nc.vector.tensor_copy(*deal_views(kw_d[:].bitcast(I32), kw_g[:].bitcast(I32), 4))
+                scores()
 
         tab_g = [tile("tab_g%d" % t, [P, S], F32) for t in range(PACK)]
         s_sb = [tile("s_sb%d" % t, [P, S], F32) for t in range(PACK)]
@@ -191,6 +201,11 @@ def tile_picked_jkeybondkindaharm_none_po_kernel(
             nc.vector.tensor_tensor(out=weave_out(woven[:]), in0=weave_in(prod[:]), in1=weave_in(t4[:]), op=ALU.add)
             nc.vector.quantize_mx(out=z2_w[:, start : start + width].bitcast(FP8X4), scales=z2_s[:, start : start + width], in_=woven[:])
 
+        w2w_d = tile("w2w_d", [P, S], U32)
+        w3w_d = tile("w3w_d", [P, S], U32)
+        nc.scalar.copy(*deal_views(w2w_d[:], w2w[:], 4))
+        nc.scalar.copy(*deal_views(w3w_d[:], w3w[:], 4))
+
         z2_chunk(0)
         for t in range(PACK):
             nc.vector.tensor_scalar(out=z_planes[:, t, :], in0=dts[t][:], scalar1=gn_sb[:, t : t + 1], scalar2=None, op0=ALU.mult)
@@ -200,11 +215,6 @@ def tile_picked_jkeybondkindaharm_none_po_kernel(
         nc.vector.tensor_copy(*deal_views(w23s_d[:], w23s[:], 16))
         nc.vector.quantize_mx(out=z_w[:].bitcast(FP8X4), scales=z_s[:], in_=z_woven[:])
         z2_chunk(1)
-
-        w2w_d = tile("w2w_d", [P, S], U32)
-        w3w_d = tile("w3w_d", [P, S], U32)
-        nc.scalar.copy(*deal_views(w2w_d[:], w2w[:], 4))
-        nc.scalar.copy(*deal_views(w3w_d[:], w3w[:], 4))
 
         h_ps = [psum.tile([P, S], F32, name="h_ps%d" % t, tag="bank%d" % t) for t in range(PACK)]
         for t in range(PACK):
@@ -225,6 +235,9 @@ def tile_picked_jkeybondkindaharm_none_po_kernel(
             else:
                 nc.vector.tensor_copy(out=h_sb[:, t, :], in_=h_ps[t][:])
 
+        h_sq = tile("h_sq", [P, PACK, S], F32)
+        for t in range(PACK):
+            nc.scalar.activation(out=h_sq[:, t, :], in_=h_ps[t][:], func=ACT.Square)
         out_w = tile("out_w", [P, S], U32)
         out_s = tile("out_s", [P, S], U8)
         out_rows = out_0.rearrange("(p t) j -> p t j", t=PACK)
@@ -236,20 +249,18 @@ def tile_picked_jkeybondkindaharm_none_po_kernel(
             other_sq = tile("other_sq%d" % c, shape, F32)
             num = tile("num%d" % c, shape, F32)
             squares = tile("squares%d" % c, shape, F32)
-            root = tile("root%d" % c, shape, F32)
+            root = tile("root%d" % c, shape, F32, "root")
             inverse = tile("inverse%d" % c, shape, F32)
             result = tile("result%d" % c, shape, F32)
             woven = tile("out_woven%d" % c, [P, PACK * width], BF16)
-            h_sq = tile("h_sq%d" % c, shape, F32)
             for t in range(PACK):
-                if t % 2:
+                if c == 1 and t % 2:
                     nc.scalar.activation(out=other[:, t, :], in_=h_sb[:, t, :].indirect(entries(n6_l, start, width)), func=ACT.Copy)
                 else:
                     nc.vector.tensor_copy(out=other[:, t, :], in_=h_sb[:, t, :].indirect(entries(n6_l, start, width)))
-            nc.scalar.activation(out=h_sq[:], in_=h_sb[:, :, span], func=ACT.Square)
             nc.scalar.activation(out=other_sq[:], in_=other[:], func=ACT.Square)
             nc.vector.tensor_tensor(out=num[:], in0=other[:], in1=h_sb[:, :, span], op=ALU.mult)
-            nc.vector.tensor_tensor(out=squares[:], in0=other_sq[:], in1=h_sq[:], op=ALU.add)
+            nc.vector.tensor_tensor(out=squares[:], in0=other_sq[:], in1=h_sq[:, :, span], op=ALU.add)
             nc.scalar.activation(out=root[:], in_=squares[:], func=ACT.Abs_reciprocal_sqrt, scale=0.5, bias=quarter[:])
             nc.scalar.activation(out=inverse[:], in_=root[:], func=ACT.Square)
             nc.vector.tensor_tensor(out=result[:], in0=num[:], in1=inverse[:], op=ALU.mult)

@@ -86,6 +86,8 @@ def tile_picked_jkeybondkindaharm_none_po_kernel(
             nc.vector.memset(plane[:].bitcast(I32), 0)
         nc.vector.memset(quarter[:], 0.25)
 
+        warm = tile("warm", [P, 1], F32)
+        nc.scalar.activation(out=warm[:], in_=quarter[:], func=ACT.Abs_reciprocal_sqrt)
         tab_rows = tab.rearrange("(p t) j -> p t j", t=PACK)
         tab_raw = [tile("tab_raw0", [P, 2, S], F32)]
         gk_sb = tile("gk_sb", [P, PACK], F32)

@@ -13,14 +13,25 @@ ACT = mybir.ActivationFunctionType
 ALU = mybir.AluOpType
 
 P = 128
-PACK = 4
+PLANES = 4
+QUADRANTS = 4
 S = 512
 T = 1024
 G = 2048
 PAIRS = 256
-FLOPS = 4 * 2 * 512 * 512 * 512
-Z2_CHUNKS = ((0, 256), (256, 256))
-OUT_CHUNKS = ((0, 256), (256, 256))
+HALF = S // 2
+FLOPS = 4 * 2 * S * S * S
+
+LINE_WORDS = 4
+LINE_BYTES = 16
+PLANE_BYTES = 4 * S
+
+KEY_SCALE_FIRST = 14
+W3_SCALE_FIRST = 4
+
+EARLY_TAB_PLANES = 2
+SCALAR_Z_PLANES = 2
+OUT_PIECES = ((0, HALF), (HALF, HALF // 2), (HALF + HALF // 2, HALF // 2))
 
 
 def words_view(words):
@@ -28,23 +39,26 @@ def words_view(words):
 
 
 def load_scale_rows(queue, plane, scales, first):
-    for q in range(4):
-        queue.dma_start(out=plane[32 * q + first : 32 * q + first + 4, :].bitcast(I32), in_=scales[0, 4 * q : 4 * q + 4, :].bitcast(I32))
+    for q in range(QUADRANTS):
+        queue.dma_start(
+            out=plane[32 * q + first : 32 * q + first + 4, :].bitcast(I32),
+            in_=scales[0, 4 * q : 4 * q + 4, :].bitcast(I32),
+        )
 
 
-def deal_views(dealt, plain, run):
+def deal_views(dealt, plain, line):
     return (
-        dealt.rearrange("p (t b i) -> p b t i", t=PACK, i=run),
-        plain.rearrange("p (b i t) -> p b t i", t=PACK, i=run),
+        dealt.rearrange("p (t b i) -> p b t i", t=PLANES, i=line),
+        plain.rearrange("p (b i t) -> p b t i", t=PLANES, i=line),
     )
 
 
-def weave_out(woven):
-    return woven.rearrange("p (c i t) -> p c t i", t=PACK, i=4)
+def woven_view(woven):
+    return woven.rearrange("p (c i t) -> p c t i", t=PLANES, i=LINE_WORDS)
 
 
-def weave_in(planes):
-    return planes.rearrange("p t (c i) -> p c t i", i=4)
+def planes_view(planes):
+    return planes.rearrange("p t (c i) -> p c t i", i=LINE_WORDS)
 
 
 def entries(offsets, start, count):
@@ -58,218 +72,242 @@ def tile_picked_jkeybondkindaharm_none_po_kernel(
     nc = tc.nc
     with ExitStack() as ctx:
         lists = ctx.enter_context(tc.tile_pool(name="lists", bufs=1))
-        sb = ctx.enter_context(tc.tile_pool(name="sb", bufs=1))
-        turn = ctx.enter_context(tc.tile_pool(name="turn", bufs=1))
+        held = ctx.enter_context(tc.tile_pool(name="held", bufs=1))
+        placed = ctx.enter_context(tc.tile_pool(name="placed", bufs=1))
         psum = ctx.enter_context(tc.psum_pool(name="psum", bufs=1))
 
-        def tile(name, shape, dtype, tag=None):
-            return sb.tile(shape, dtype, name=name, tag=tag or name, align_bytes=64)
+        def tile(name, shape, dtype, after=None):
+            return held.tile(shape, dtype, name=name, tag=after or name, align_bytes=64)
 
-        def in_turn(name, shape, dtype, offset):
-            return turn.tile(shape, dtype, name=name, align_bytes=64, offset=offset)
+        def tile_at(name, shape, dtype, offset):
+            return placed.tile(shape, dtype, name=name, align_bytes=64, offset=offset)
 
         def load_list(name, source):
             offsets = lists.tile(list(source.shape), U16, name=name)
             nc.sync.dma_start(offsets[:], source)
             return offsets
 
-        xw = tile("xw", [P, T], U32)
-        xs = tile("xs", [P, T], U8)
-        dw = tile("dw", [P, G], U32)
-        ds = tile("ds", [P, G], U8)
-        w1w = tile("w1w", [P, S], U32)
-        w1s = tile("w1s", [P, S], U8)
-        key_scales = tile("key_scales", [P, S], U8)
+        def gather_on_scalar(out, window, offsets):
+            nc.scalar.activation(out=out, in_=window.indirect(offsets), func=ACT.Copy)
+
+        def product(out, words, scales, t, moving_words, moving_scales, start, stop):
+            cols = slice(P * t, P * (t + 1))
+            nc.tensor.matmul_mx(
+                out=out, lhsT=words[:, cols].bitcast(FP8X4), lhsT_scale=scales[:, cols],
+                rhs=moving_words.bitcast(FP8X4), rhs_scale=moving_scales, start=start, stop=stop,
+            )
+
+        x_w = tile("x_w", [P, T], U32)
+        x_s = tile("x_s", [P, T], U8)
+        d_w = tile("d_w", [P, G], U32)
+        d_s = tile("d_s", [P, G], U8)
+        w1_w = tile("w1_w", [P, S], U32)
+        w1_s = tile("w1_s", [P, S], U8)
+        key_s = tile("key_s", [P, S], U8)
         quarter = tile("quarter", [P, 1], F32)
-        nc.gpsimd.memset(ds[:].bitcast(I32), 0)
-        for plane in (xs, w1s, key_scales):
-            nc.vector.memset(plane[:].bitcast(I32), 0)
+        nc.gpsimd.memset(d_s[:].bitcast(I32), 0)
+        for scale_tile in (x_s, w1_s, key_s):
+            nc.vector.memset(scale_tile[:].bitcast(I32), 0)
         nc.vector.memset(quarter[:], 0.25)
 
-        warm = tile("warm", [P, 1], F32)
-        nc.scalar.activation(out=warm[:], in_=quarter[:], func=ACT.Abs_reciprocal_sqrt)
-        tab_rows = tab.rearrange("(p t) j -> p t j", t=PACK)
-        tab_raw = [tile("tab_raw0", [P, 2, S], F32)]
-        gk_sb = tile("gk_sb", [P, PACK], F32)
+        warm_up = tile("warm_up", [P, 1], F32)
+        nc.scalar.activation(out=warm_up[:], in_=quarter[:], func=ACT.Abs_reciprocal_sqrt)
 
-        load_scale_rows(nc.gpsimd, ds, d_scales, 14)
+        tab_rows = tab.rearrange("(p t) j -> p t j", t=PLANES)
+        tab_early = tile("tab_early", [P, EARLY_TAB_PLANES, S], F32)
+        gk_sb = tile("gk_sb", [P, PLANES], F32)
+
+        load_scale_rows(nc.gpsimd, d_s, d_scales, KEY_SCALE_FIRST)
         offs_l = load_list("offs_l", offs)
-        nc.sync.dma_start(out=xw[:].bitcast(I32), in_=words_view(x_words))
+        nc.sync.dma_start(out=x_w[:].bitcast(I32), in_=words_view(x_words))
         two_l = load_list("two_l", two)
-        nc.sync.dma_start(out=w1w[:].bitcast(I32), in_=words_view(w1_words))
-        nc.sync.dma_start(out=tab_raw[0][:], in_=tab_rows[:, 0:2, :])
-        nc.sync.dma_start(out=gk_sb[:], in_=gk.rearrange("(p t) o -> p (t o)", t=PACK))
+        nc.sync.dma_start(out=w1_w[:].bitcast(I32), in_=words_view(w1_words))
+        nc.sync.dma_start(out=tab_early[:], in_=tab_rows[:, :EARLY_TAB_PLANES, :])
+        nc.sync.dma_start(out=gk_sb[:], in_=gk.rearrange("(p t) o -> p (t o)", t=PLANES))
         n3_l = load_list("n3_l", n3)
         n4_l = load_list("n4_l", n4)
-        load_scale_rows(nc.sync, xs, x_scales, 0)
-        load_scale_rows(nc.sync, w1s, w1_scales, 0)
+        load_scale_rows(nc.sync, x_s, x_scales, 0)
+        load_scale_rows(nc.sync, w1_s, w1_scales, 0)
         n1_l = load_list("n1_l", n1)
         n2_l = load_list("n2_l", n2)
         kidx_l = load_list("kidx_l", kidx)
-        nc.sync.dma_start(out=dw[:].bitcast(I32), in_=words_view(d_words))
+        nc.sync.dma_start(out=d_w[:].bitcast(I32), in_=words_view(d_words))
         n5_l = load_list("n5_l", n5)
         n6_l = load_list("n6_l", n6)
 
-        xa_w = tile("xa_w", [P, S], U32)
-        xa_s = tile("xa_s", [P, S], U8)
-        nc.vector.tensor_copy(out=xa_w[:], in_=xw[:].indirect(offs_l[:]))
-        nc.vector.tensor_copy(out=xa_s[:], in_=xs[:].indirect(offs_l[:]))
-        w1w_d = tile("w1w_d", [P, S], U32)
-        w1s_d = tile("w1s_d", [P, S], U8)
-        nc.scalar.copy(*deal_views(w1w_d[:], w1w[:], 4))
-        nc.vector.tensor_copy(*deal_views(w1s_d[:], w1s[:], 16))
-        tab_raw.append(tile("tab_raw1", [P, 2, S], F32, "w1w"))
-        nc.sync.dma_start(out=tab_raw[1][:], in_=tab_rows[:, 2:4, :])
-        y_ps = [psum.tile([P, S], F32, name="y_ps%d" % t, tag="bank%d" % t) for t in range(PACK)]
-        for t in range(PACK):
-            cols = slice(P * t, P * (t + 1))
-            nc.tensor.matmul_mx(out=y_ps[t][:], lhsT=w1w_d[:, cols].bitcast(FP8X4), lhsT_scale=w1s_d[:, cols],
-                                rhs=xa_w[:].bitcast(FP8X4), rhs_scale=xa_s[:], start=True, stop=True)
+        xi_w = tile("xi_w", [P, S], U32)
+        xi_s = tile("xi_s", [P, S], U8)
+        nc.vector.tensor_copy(out=xi_w[:], in_=x_w[:].indirect(offs_l[:]))
+        nc.vector.tensor_copy(out=xi_s[:], in_=x_s[:].indirect(offs_l[:]))
+        w1_w_dealt = tile("w1_w_dealt", [P, S], U32)
+        w1_s_dealt = tile("w1_s_dealt", [P, S], U8)
+        nc.scalar.copy(*deal_views(w1_w_dealt[:], w1_w[:], LINE_WORDS))
+        nc.vector.tensor_copy(*deal_views(w1_s_dealt[:], w1_s[:], LINE_BYTES))
+        tab_late = tile("tab_late", [P, PLANES - EARLY_TAB_PLANES, S], F32, after="w1_w")
+        nc.sync.dma_start(out=tab_late[:], in_=tab_rows[:, EARLY_TAB_PLANES:, :])
+        y_ps = [psum.tile([P, S], F32, name="y_ps%d" % t, tag="bank%d" % t) for t in range(PLANES)]
+        for t in range(PLANES):
+            product(y_ps[t][:], w1_w_dealt, w1_s_dealt, t, xi_w[:], xi_s[:], True, True)
 
-        xb_w = tile("xb_w", [P, S], U32)
-        nc.vector.tensor_copy(out=xb_w[:], in_=xw[:].indirect(two_l[:]))
-        xb_s = tile("xb_s", [P, S], U8)
-        nc.vector.tensor_copy(out=xb_s[:], in_=xs[:].indirect(two_l[:]))
-        ks_g = in_turn("ks_g", [P, S], U8, 0)
-        ks_d = tile("ks_d", [P, S], U8)
-        nc.vector.tensor_copy(out=ks_g[:], in_=ds[:].indirect(kidx_l[:]))
-        nc.vector.tensor_copy(*deal_views(ks_d[:], ks_g[:], 16))
-        for q in range(4):
-            nc.sync.dma_start(out=key_scales[32 * q : 32 * q + 4, :].bitcast(I32), in_=ks_d[32 * q + 14 : 32 * q + 18, :].bitcast(I32))
-        gn_sb = tile("gn_sb", [P, PACK], F32, "xs")
-        nc.sync.dma_start(out=gn_sb[:], in_=gn.rearrange("(p t) o -> p (t o)", t=PACK))
-        w23s = tile("w23s", [P, S], U8, "ds")
-        nc.gpsimd.memset(w23s[:].bitcast(I32), 0)
-        load_scale_rows(nc.sync, w23s, w2_scales, 0)
-        load_scale_rows(nc.sync, w23s, w3_scales, 4)
-        s_ps = [psum.tile([P, S], F32, name="s_ps%d" % t, tag="bank%d" % (PACK + t)) for t in range(PACK)]
+        xt_w = tile("xt_w", [P, S], U32)
+        nc.vector.tensor_copy(out=xt_w[:], in_=x_w[:].indirect(two_l[:]))
+        xt_s = tile("xt_s", [P, S], U8)
+        key_s_picked = tile_at("key_s_picked", [P, S], U8, 0)
+        key_s_dealt = tile("key_s_dealt", [P, S], U8)
+        nc.vector.tensor_copy(out=key_s_picked[:], in_=d_s[:].indirect(kidx_l[:]))
+        nc.vector.tensor_copy(out=xt_s[:], in_=x_s[:].indirect(two_l[:]))
+        nc.vector.tensor_copy(*deal_views(key_s_dealt[:], key_s_picked[:], LINE_BYTES))
+        for q in range(QUADRANTS):
+            source = 32 * q + KEY_SCALE_FIRST
+            nc.sync.dma_start(
+                out=key_s[32 * q : 32 * q + 4, :].bitcast(I32), in_=key_s_dealt[source : source + 4, :].bitcast(I32)
+            )
+        gn_sb = tile("gn_sb", [P, PLANES], F32, after="x_s")
+        nc.sync.dma_start(out=gn_sb[:], in_=gn.rearrange("(p t) o -> p (t o)", t=PLANES))
+        w23_s = tile("w23_s", [P, S], U8, after="d_s")
+        nc.gpsimd.memset(w23_s[:].bitcast(I32), 0)
+        load_scale_rows(nc.sync, w23_s, w2_scales, 0)
+        load_scale_rows(nc.sync, w23_s, w3_scales, W3_SCALE_FIRST)
+        s_ps = [psum.tile([P, S], F32, name="s_ps%d" % t, tag="bank%d" % (PLANES + t)) for t in range(PLANES)]
 
-        def scores():
-            for t in range(PACK):
-                cols = slice(P * t, P * (t + 1))
-                nc.tensor.matmul_mx(out=s_ps[t][:], lhsT=kw_d[:, cols].bitcast(FP8X4), lhsT_scale=key_scales[:, cols],
-                                    rhs=xb_w[:].bitcast(FP8X4), rhs_scale=xb_s[:], start=True, stop=True)
+        tab_g = [tile("tab_g%d" % t, [P, S], F32) for t in range(PLANES)]
+        factor = [tile("factor0", [P, PLANES, HALF], F32)]
+        addend = [tile("addend0", [P, PLANES, HALF], F32)]
+        for t in range(EARLY_TAB_PLANES):
+            nc.scalar.activation(out=tab_g[t][:], in_=tab_early[:, t, :], func=ACT.Copy, scale=gk_sb[:, t : t + 1])
+        for t in range(EARLY_TAB_PLANES):
+            gather_on_scalar(factor[0][:, t, :], tab_g[t][:], entries(n3_l, 0, HALF))
+            gather_on_scalar(addend[0][:, t, :], tab_g[t][:], entries(n4_l, 0, HALF))
 
-        z_planes = tile("z_planes", [P, PACK, S], BF16)
-        dts = []
-        for t in range(PACK):
+        dt = []
+        for t in range(PLANES):
             y_sb = tile("y_sb%d" % t, [P, S], F32)
-            pa = in_turn("pa%d" % t, [P, PAIRS], F32, 2048 * (t + 2))
-            pb = in_turn("pb%d" % t, [P, PAIRS], F32, 2048 * (t + 2) + 1024)
-            dt_sb = in_turn("dt_sb%d" % t, [P, S], F32, 2048 * t)
+            pa = tile_at("pa%d" % t, [P, PAIRS], F32, PLANE_BYTES * (t + 2))
+            pb = tile_at("pb%d" % t, [P, PAIRS], F32, PLANE_BYTES * (t + 2) + PLANE_BYTES // 2)
+            dt.append(tile_at("dt%d" % t, [P, S], F32, PLANE_BYTES * t))
             nc.scalar.copy(out=y_sb[:], in_=y_ps[t][:])
-            nc.scalar.activation(out=pa[:], in_=y_sb[:].indirect(n1_l[:]), func=ACT.Copy)
-            nc.scalar.activation(out=pb[:], in_=y_sb[:].indirect(n2_l[:]), func=ACT.Copy)
-            nc.vector.tensor_tensor(out=dt_sb[:].indirect(n1_l[:]), in0=pa[:], in1=pb[:], op=ALU.add)
-            nc.vector.tensor_tensor(out=dt_sb[:].indirect(n2_l[:]), in0=pa[:], in1=pb[:], op=ALU.mult)
-            dts.append(dt_sb)
+            gather_on_scalar(pa[:], y_sb[:], n1_l[:])
+            gather_on_scalar(pb[:], y_sb[:], n2_l[:])
+            nc.vector.tensor_tensor(out=dt[t][:].indirect(n1_l[:]), in0=pa[:], in1=pb[:], op=ALU.add)
+            nc.vector.tensor_tensor(out=dt[t][:].indirect(n2_l[:]), in0=pa[:], in1=pb[:], op=ALU.mult)
             if t == 0:
-                kw_g = in_turn("kw_g", [P, S], U32, 3072)
-                kw_d = tile("kw_d", [P, S], U32)
-                nc.vector.tensor_copy(out=kw_g[:], in_=dw[:].indirect(kidx_l[:]))
-                nc.vector.tensor_copy(*deal_views(kw_d[:].bitcast(I32), kw_g[:].bitcast(I32), 4))
-                scores()
+                key_w_picked = tile_at("key_w_picked", [P, S], U32, PLANE_BYTES + PLANE_BYTES // 2)
+                key_w = tile("key_w", [P, S], U32)
+                nc.vector.tensor_copy(out=key_w_picked[:], in_=d_w[:].indirect(kidx_l[:]))
+                nc.vector.tensor_copy(*deal_views(key_w[:].bitcast(I32), key_w_picked[:].bitcast(I32), LINE_WORDS))
+                for u in range(PLANES):
+                    product(s_ps[u][:], key_w, key_s, u, xt_w[:], xt_s[:], True, True)
 
-        tab_g = [tile("tab_g%d" % t, [P, S], F32) for t in range(PACK)]
-        s_sb = [tile("s_sb%d" % t, [P, S], F32) for t in range(PACK)]
-        for t in range(PACK):
+        s_sb = [tile("s_sb%d" % t, [P, S], F32) for t in range(PLANES)]
+        for t in range(PLANES):
             nc.scalar.activation(out=s_sb[t][:], in_=s_ps[t][:], func=ACT.Copy, scale=0.0625)
-        for t in range(PACK):
-            nc.scalar.activation(out=tab_g[t][:], in_=tab_raw[t // 2][:, t % 2, :], func=ACT.Copy, scale=gk_sb[:, t : t + 1])
+        for t in range(EARLY_TAB_PLANES, PLANES):
+            nc.scalar.activation(
+                out=tab_g[t][:], in_=tab_late[:, t - EARLY_TAB_PLANES, :], func=ACT.Copy, scale=gk_sb[:, t : t + 1]
+            )
 
-        w2w = tile("w2w", [P, S], U32, "tab_raw0")
-        w3w = tile("w3w", [P, S], U32, "xw")
-        nc.sync.dma_start(out=w2w[:].bitcast(I32), in_=words_view(w2_words))
-        nc.sync.dma_start(out=w3w[:].bitcast(I32), in_=words_view(w3_words))
+        w2_w = tile("w2_w", [P, S], U32, after="tab_early")
+        w3_w = tile("w3_w", [P, S], U32, after="x_w")
+        nc.sync.dma_start(out=w2_w[:].bitcast(I32), in_=words_view(w2_words))
+        nc.sync.dma_start(out=w3_w[:].bitcast(I32), in_=words_view(w3_words))
         z2_w = tile("z2_w", [P, S], U32)
         z2_s = tile("z2_s", [P, S], U8)
         z_w = tile("z_w", [P, S], U32)
         z_s = tile("z_s", [P, S], U8)
+        w2_w_dealt = tile("w2_w_dealt", [P, S], U32)
+        w3_w_dealt = tile("w3_w_dealt", [P, S], U32)
+        nc.scalar.copy(*deal_views(w2_w_dealt[:], w2_w[:], LINE_WORDS))
+        nc.scalar.copy(*deal_views(w3_w_dealt[:], w3_w[:], LINE_WORDS))
 
-        def z2_chunk(c):
-            start, width = Z2_CHUNKS[c]
-            s5 = tile("s5_%d" % c, [P, PACK, width], F32)
-            t3 = tile("t3_%d" % c, [P, PACK, width], F32, "y_sb0" if c == 1 else None)
-            t4 = tile("t4_%d" % c, [P, PACK, width], F32, "s_sb3" if c == 1 else None)
-            prod = tile("prod_%d" % c, [P, PACK, width], F32)
-            woven = tile("z2_woven%d" % c, [P, PACK * width], BF16)
-            for t in range(PACK):
-                nc.scalar.activation(out=s5[:, t, :], in_=s_sb[t][:].indirect(entries(n5_l, start, width)), func=ACT.Copy)
-            for t in range(PACK):
-                nc.scalar.activation(out=t3[:, t, :], in_=tab_g[t][:].indirect(entries(n3_l, start, width)), func=ACT.Copy)
-            for t in range(PACK):
-                nc.scalar.activation(out=t4[:, t, :], in_=tab_g[t][:].indirect(entries(n4_l, start, width)), func=ACT.Copy)
-            nc.vector.tensor_tensor(out=prod[:], in0=s5[:], in1=t3[:], op=ALU.mult)
-            nc.vector.tensor_tensor(out=weave_out(woven[:]), in0=weave_in(prod[:]), in1=weave_in(t4[:]), op=ALU.add)
-            nc.vector.quantize_mx(out=z2_w[:, start : start + width].bitcast(FP8X4), scales=z2_s[:, start : start + width], in_=woven[:])
-
-        w2w_d = tile("w2w_d", [P, S], U32)
-        w3w_d = tile("w3w_d", [P, S], U32)
-        nc.scalar.copy(*deal_views(w2w_d[:], w2w[:], 4))
-        nc.scalar.copy(*deal_views(w3w_d[:], w3w[:], 4))
-
-        z2_chunk(0)
-        for t in range(PACK):
-            nc.vector.tensor_scalar(out=z_planes[:, t, :], in0=dts[t][:], scalar1=gn_sb[:, t : t + 1], scalar2=None, op0=ALU.mult)
-        z_woven = tile("z_woven", [P, PACK * S], BF16)
-        nc.vector.tensor_copy(out=weave_out(z_woven[:]), in_=weave_in(z_planes[:]))
-        w23s_d = tile("w23s_d", [P, S], U8)
-        nc.vector.tensor_copy(*deal_views(w23s_d[:], w23s[:], 16))
-        nc.vector.quantize_mx(out=z_w[:].bitcast(FP8X4), scales=z_s[:], in_=z_woven[:])
-        z2_chunk(1)
-
-        h_ps = [psum.tile([P, S], F32, name="h_ps%d" % t, tag="bank%d" % t) for t in range(PACK)]
-        for t in range(PACK):
-            cols = slice(P * t, P * (t + 1))
-            nc.tensor.matmul_mx(out=h_ps[t][:], lhsT=w2w_d[:, cols].bitcast(FP8X4), lhsT_scale=w23s_d[:, cols],
-                                rhs=z_w[:].bitcast(FP8X4), rhs_scale=z_s[:], start=True, stop=False)
-        for c, (start, width) in enumerate(Z2_CHUNKS):
-            span = slice(start, start + width)
-            for t in range(PACK):
-                cols = slice(P * t, P * (t + 1))
-                nc.tensor.matmul_mx(out=h_ps[t][:, span], lhsT=w3w_d[:, cols].bitcast(FP8X4), lhsT_scale=w23s_d[4:P, cols],
-                                    rhs=z2_w[:, span].bitcast(FP8X4), rhs_scale=z2_s[:, span], start=False, stop=(c == len(Z2_CHUNKS) - 1))
-
-        h_sb = tile("h_sb", [P, PACK, S], F32)
-        for t in range(PACK):
-            if t % 2:
-                nc.scalar.copy(out=h_sb[:, t, :], in_=h_ps[t][:])
+        z_planes = tile("z_planes", [P, PLANES, S], BF16, after="key_w")
+        for t in range(PLANES):
+            gain = gn_sb[:, t : t + 1]
+            if t < SCALAR_Z_PLANES:
+                nc.scalar.activation(out=z_planes[:, t, :], in_=dt[t][:], func=ACT.Copy, scale=gain)
             else:
-                nc.vector.tensor_copy(out=h_sb[:, t, :], in_=h_ps[t][:])
+                nc.vector.tensor_scalar(out=z_planes[:, t, :], in0=dt[t][:], scalar1=gain, scalar2=None, op0=ALU.mult)
+        z_woven = tile("z_woven", [P, PLANES * S], BF16)
+        nc.vector.tensor_copy(out=woven_view(z_woven[:]), in_=planes_view(z_planes[:]))
+        w23_s_dealt = tile("w23_s_dealt", [P, S], U8)
+        nc.vector.tensor_copy(*deal_views(w23_s_dealt[:], w23_s[:], LINE_BYTES))
+        nc.vector.quantize_mx(out=z_w[:].bitcast(FP8X4), scales=z_s[:], in_=z_woven[:])
 
-        h_sq = tile("h_sq", [P, PACK, S], F32)
-        for t in range(PACK):
-            nc.scalar.activation(out=h_sq[:, t, :], in_=h_ps[t][:], func=ACT.Square)
+        for half in range(2):
+            start = HALF * half
+            span = slice(start, start + HALF)
+            picked_s = tile("picked_s%d" % half, [P, PLANES, HALF], F32)
+            if half:
+                factor.append(tile("factor1", [P, PLANES, HALF], F32, after="y_sb0"))
+                addend.append(tile("addend1", [P, PLANES, HALF], F32, after="s_sb%d" % (PLANES - 1)))
+            scaled = tile("scaled%d" % half, [P, PLANES, HALF], F32)
+            z2_woven = tile("z2_woven%d" % half, [P, PLANES * HALF], BF16)
+            tab_planes_left = range(0 if half else EARLY_TAB_PLANES, PLANES)
+            for t in range(PLANES):
+                gather_on_scalar(picked_s[:, t, :], s_sb[t][:], entries(n5_l, start, HALF))
+            for t in tab_planes_left:
+                gather_on_scalar(factor[half][:, t, :], tab_g[t][:], entries(n3_l, start, HALF))
+            for t in tab_planes_left:
+                gather_on_scalar(addend[half][:, t, :], tab_g[t][:], entries(n4_l, start, HALF))
+            nc.vector.tensor_tensor(out=scaled[:], in0=picked_s[:], in1=factor[half][:], op=ALU.mult)
+            nc.vector.tensor_tensor(
+                out=woven_view(z2_woven[:]), in0=planes_view(scaled[:]), in1=planes_view(addend[half][:]), op=ALU.add
+            )
+            nc.vector.quantize_mx(out=z2_w[:, span].bitcast(FP8X4), scales=z2_s[:, span], in_=z2_woven[:])
+
+        h = tile("h", [P, PLANES, S], F32)
+        h_sq = tile("h_sq", [P, PLANES, S], F32)
+        for half in range(2):
+            span = slice(HALF * half, HALF * (half + 1))
+            h_ps = [
+                psum.tile([P, HALF], F32, name="h_ps%d_%d" % (half, t), tag="bank%d" % (PLANES * half + t))
+                for t in range(PLANES)
+            ]
+            for t in range(PLANES):
+                product(h_ps[t][:], w2_w_dealt, w23_s_dealt, t, z_w[:, span], z_s[:, span], True, False)
+            for t in range(PLANES):
+                product(h_ps[t][:], w3_w_dealt, w23_s_dealt[W3_SCALE_FIRST:P, :], t, z2_w[:, span], z2_s[:, span], False, True)
+            for t in range(PLANES):
+                if half:
+                    nc.vector.tensor_copy(out=h[:, t, span], in_=h_ps[t][:])
+                else:
+                    nc.scalar.copy(out=h[:, t, span], in_=h_ps[t][:])
+            if half == 0:
+                nc.scalar.activation(out=h_sq[:, :, span], in_=h[:, :, span], func=ACT.Square)
+
         out_w = tile("out_w", [P, S], U32)
         out_s = tile("out_s", [P, S], U8)
-        out_rows = out_0.rearrange("(p t) j -> p t j", t=PACK)
+        out_rows = out_0.rearrange("(p t) j -> p t j", t=PLANES)
         out_words = words_view(out_1)
-        for c, (start, width) in enumerate(OUT_CHUNKS):
+        for piece, (start, width) in enumerate(OUT_PIECES):
             span = slice(start, start + width)
-            shape = [P, PACK, width]
-            other = tile("other%d" % c, shape, F32)
-            other_sq = tile("other_sq%d" % c, shape, F32)
-            num = tile("num%d" % c, shape, F32)
-            squares = tile("squares%d" % c, shape, F32)
-            root = tile("root%d" % c, shape, F32, "root")
-            inverse = tile("inverse%d" % c, shape, F32)
-            result = tile("result%d" % c, shape, F32)
-            woven = tile("out_woven%d" % c, [P, PACK * width], BF16)
-            for t in range(PACK):
-                if c == 1 and t % 2:
-                    nc.scalar.activation(out=other[:, t, :], in_=h_sb[:, t, :].indirect(entries(n6_l, start, width)), func=ACT.Copy)
+            shape = [P, PLANES, width]
+            pa2 = tile("pa2_%d" % piece, shape, F32)
+            pa2_sq = tile("pa2_sq%d" % piece, shape, F32)
+            cross = tile("cross%d" % piece, shape, F32)
+            squares = tile("squares%d" % piece, shape, F32)
+            root = tile("root%d" % piece, shape, F32, after="root")
+            inverse = tile("inverse%d" % piece, shape, F32)
+            result = tile("result%d" % piece, shape, F32)
+            out_woven = tile("out_woven%d" % piece, [P, PLANES * width], BF16)
+            for t in range(PLANES):
+                if t % 2:
+                    gather_on_scalar(pa2[:, t, :], h[:, t, :], entries(n6_l, start, width))
                 else:
-                    nc.vector.tensor_copy(out=other[:, t, :], in_=h_sb[:, t, :].indirect(entries(n6_l, start, width)))
-            nc.scalar.activation(out=other_sq[:], in_=other[:], func=ACT.Square)
-            nc.vector.tensor_tensor(out=num[:], in0=other[:], in1=h_sb[:, :, span], op=ALU.mult)
-            nc.vector.tensor_tensor(out=squares[:], in0=other_sq[:], in1=h_sq[:, :, span], op=ALU.add)
+                    nc.vector.tensor_copy(out=pa2[:, t, :], in_=h[:, t, :].indirect(entries(n6_l, start, width)))
+            if start >= HALF:
+                nc.scalar.activation(out=h_sq[:, :, span], in_=h[:, :, span], func=ACT.Square)
+            nc.scalar.activation(out=pa2_sq[:], in_=pa2[:], func=ACT.Square)
+            nc.vector.tensor_tensor(out=cross[:], in0=pa2[:], in1=h[:, :, span], op=ALU.mult)
+            nc.vector.tensor_tensor(out=squares[:], in0=pa2_sq[:], in1=h_sq[:, :, span], op=ALU.add)
             nc.scalar.activation(out=root[:], in_=squares[:], func=ACT.Abs_reciprocal_sqrt, scale=0.5, bias=quarter[:])
             nc.scalar.activation(out=inverse[:], in_=root[:], func=ACT.Square)
-            nc.vector.tensor_tensor(out=result[:], in0=num[:], in1=inverse[:], op=ALU.mult)
+            nc.vector.tensor_tensor(out=result[:], in0=cross[:], in1=inverse[:], op=ALU.mult)
             nc.sync.dma_start(out=out_rows[:, :, span], in_=result[:])
-            nc.vector.tensor_copy(out=weave_out(woven[:]), in_=weave_in(result[:]))
-            nc.vector.quantize_mx(out=out_w[:, span].bitcast(FP8X4), scales=out_s[:, span], in_=woven[:])
+            nc.vector.tensor_copy(out=woven_view(out_woven[:]), in_=planes_view(result[:]))
+            nc.vector.quantize_mx(out=out_w[:, span].bitcast(FP8X4), scales=out_s[:, span], in_=out_woven[:])
             nc.sync.dma_start(out=out_words[:, span], in_=out_w[:, span].bitcast(I32))
-        for q in range(4):
+        for q in range(QUADRANTS):
             queue = nc.scalar if q % 2 else nc.sync
-            queue.dma_start(out=out_2[0, 4 * q : 4 * q + 4, :].bitcast(I32), in_=out_s[32 * q : 32 * q + 4, :].bitcast(I32))
+            queue.dma_start(
+                out=out_2[0, 4 * q : 4 * q + 4, :].bitcast(I32), in_=out_s[32 * q : 32 * q + 4, :].bitcast(I32)
+            )

from contextlib import ExitStack

import concourse.mybir as mybir

F32 = mybir.dt.float32
BF16 = mybir.dt.bfloat16
I32 = mybir.dt.int32
U32 = mybir.dt.uint32
U16 = mybir.dt.uint16
U8 = mybir.dt.uint8
FP8X4 = mybir.dt.float8_e4m3fn_x4
ACT = mybir.ActivationFunctionType
ALU = mybir.AluOpType

P = 128
PLANES = 4
QUADRANTS = 4
S = 512
T = 1024
G = 2048
PAIRS = 256
HALF = S // 2
FLOPS = 4 * 2 * S * S * S

LINE_WORDS = 4
LINE_BYTES = 16
PLANE_BYTES = 4 * S

KEY_SCALE_FIRST = 14
W3_SCALE_FIRST = 4

EARLY_TAB_PLANES = 2
SCALAR_Z_PLANES = 2
OUT_PIECES = ((0, HALF), (HALF, HALF // 2), (HALF + HALF // 2, HALF // 2))


def words_view(words):
    return words[0].rearrange("p n t -> p (n t)").bitcast(I32)


def load_scale_rows(queue, plane, scales, first):
    for q in range(QUADRANTS):
        queue.dma_start(
            out=plane[32 * q + first : 32 * q + first + 4, :].bitcast(I32),
            in_=scales[0, 4 * q : 4 * q + 4, :].bitcast(I32),
        )


def deal_views(dealt, plain, line):
    return (
        dealt.rearrange("p (t b i) -> p b t i", t=PLANES, i=line),
        plain.rearrange("p (b i t) -> p b t i", t=PLANES, i=line),
    )


def woven_view(woven):
    return woven.rearrange("p (c i t) -> p c t i", t=PLANES, i=LINE_WORDS)


def planes_view(planes):
    return planes.rearrange("p t (c i) -> p c t i", i=LINE_WORDS)


def entries(offsets, start, count):
    return offsets[:, start // 16 : (start + count) // 16]


def tile_picked_jkeybondkindaharm_none_po_kernel(
    tc, x_words, x_scales, w1_words, w1_scales, d_words, d_scales, tab, gn, gk, w2_words, w2_scales, w3_words, w3_scales,
    offs, kidx, two, n1, n2, n3, n4, n5, n6, out_0, out_1, out_2,
):
    nc = tc.nc
    with ExitStack() as ctx:
        lists = ctx.enter_context(tc.tile_pool(name="lists", bufs=1))
        held = ctx.enter_context(tc.tile_pool(name="held", bufs=1))
        placed = ctx.enter_context(tc.tile_pool(name="placed", bufs=1))
        psum = ctx.enter_context(tc.psum_pool(name="psum", bufs=1))

        def tile(name, shape, dtype, after=None):
            return held.tile(shape, dtype, name=name, tag=after or name, align_bytes=64)

        def tile_at(name, shape, dtype, offset):
            return placed.tile(shape, dtype, name=name, align_bytes=64, offset=offset)

        def load_list(name, source):
            offsets = lists.tile(list(source.shape), U16, name=name)
            nc.sync.dma_start(offsets[:], source)
            return offsets

        def gather_on_scalar(out, window, offsets):
            nc.scalar.activation(out=out, in_=window.indirect(offsets), func=ACT.Copy)

        def product(out, words, scales, t, moving_words, moving_scales, start, stop):
            cols = slice(P * t, P * (t + 1))
            nc.tensor.matmul_mx(
                out=out, lhsT=words[:, cols].bitcast(FP8X4), lhsT_scale=scales[:, cols],
                rhs=moving_words.bitcast(FP8X4), rhs_scale=moving_scales, start=start, stop=stop,
            )

        x_w = tile("x_w", [P, T], U32)
        x_s = tile("x_s", [P, T], U8)
        d_w = tile("d_w", [P, G], U32)
        d_s = tile("d_s", [P, G], U8)
        w1_w = tile("w1_w", [P, S], U32)
        w1_s = tile("w1_s", [P, S], U8)
        key_s = tile("key_s", [P, S], U8)
        quarter = tile("quarter", [P, 1], F32)
        nc.gpsimd.memset(d_s[:].bitcast(I32), 0)
        for scale_tile in (x_s, w1_s, key_s):
            nc.vector.memset(scale_tile[:].bitcast(I32), 0)
        nc.vector.memset(quarter[:], 0.25)

        warm_up = tile("warm_up", [P, 1], F32)
        nc.scalar.activation(out=warm_up[:], in_=quarter[:], func=ACT.Abs_reciprocal_sqrt)

        tab_rows = tab.rearrange("(p t) j -> p t j", t=PLANES)
        tab_early = tile("tab_early", [P, EARLY_TAB_PLANES, S], F32)
        gk_sb = tile("gk_sb", [P, PLANES], F32)

        load_scale_rows(nc.gpsimd, d_s, d_scales, KEY_SCALE_FIRST)
        offs_l = load_list("offs_l", offs)
        nc.sync.dma_start(out=x_w[:].bitcast(I32), in_=words_view(x_words))
        two_l = load_list("two_l", two)
        nc.sync.dma_start(out=w1_w[:].bitcast(I32), in_=words_view(w1_words))
        nc.sync.dma_start(out=tab_early[:], in_=tab_rows[:, :EARLY_TAB_PLANES, :])
        nc.sync.dma_start(out=gk_sb[:], in_=gk.rearrange("(p t) o -> p (t o)", t=PLANES))
        n3_l = load_list("n3_l", n3)
        n4_l = load_list("n4_l", n4)
        load_scale_rows(nc.sync, x_s, x_scales, 0)
        load_scale_rows(nc.sync, w1_s, w1_scales, 0)
        n1_l = load_list("n1_l", n1)
        n2_l = load_list("n2_l", n2)
        kidx_l = load_list("kidx_l", kidx)
        nc.sync.dma_start(out=d_w[:].bitcast(I32), in_=words_view(d_words))
        n5_l = load_list("n5_l", n5)
        n6_l = load_list("n6_l", n6)

        xi_w = tile("xi_w", [P, S], U32)
        xi_s = tile("xi_s", [P, S], U8)
        nc.vector.tensor_copy(out=xi_w[:], in_=x_w[:].indirect(offs_l[:]))
        nc.vector.tensor_copy(out=xi_s[:], in_=x_s[:].indirect(offs_l[:]))
        w1_w_dealt = tile("w1_w_dealt", [P, S], U32)
        w1_s_dealt = tile("w1_s_dealt", [P, S], U8)
        nc.scalar.copy(*deal_views(w1_w_dealt[:], w1_w[:], LINE_WORDS))
        nc.vector.tensor_copy(*deal_views(w1_s_dealt[:], w1_s[:], LINE_BYTES))
        tab_late = tile("tab_late", [P, PLANES - EARLY_TAB_PLANES, S], F32, after="w1_w")
        nc.sync.dma_start(out=tab_late[:], in_=tab_rows[:, EARLY_TAB_PLANES:, :])
        y_ps = [psum.tile([P, S], F32, name="y_ps%d" % t, tag="bank%d" % t) for t in range(PLANES)]
        for t in range(PLANES):
            product(y_ps[t][:], w1_w_dealt, w1_s_dealt, t, xi_w[:], xi_s[:], True, True)

        xt_w = tile("xt_w", [P, S], U32)
        nc.vector.tensor_copy(out=xt_w[:], in_=x_w[:].indirect(two_l[:]))
        xt_s = tile("xt_s", [P, S], U8)
        key_s_picked = tile_at("key_s_picked", [P, S], U8, 0)
        key_s_dealt = tile("key_s_dealt", [P, S], U8)
        nc.vector.tensor_copy(out=key_s_picked[:], in_=d_s[:].indirect(kidx_l[:]))
        nc.vector.tensor_copy(out=xt_s[:], in_=x_s[:].indirect(two_l[:]))
        nc.vector.tensor_copy(*deal_views(key_s_dealt[:], key_s_picked[:], LINE_BYTES))
        for q in range(QUADRANTS):
            source = 32 * q + KEY_SCALE_FIRST
            nc.sync.dma_start(
                out=key_s[32 * q : 32 * q + 4, :].bitcast(I32), in_=key_s_dealt[source : source + 4, :].bitcast(I32)
            )
        gn_sb = tile("gn_sb", [P, PLANES], F32, after="x_s")
        nc.sync.dma_start(out=gn_sb[:], in_=gn.rearrange("(p t) o -> p (t o)", t=PLANES))
        w23_s = tile("w23_s", [P, S], U8, after="d_s")
        nc.gpsimd.memset(w23_s[:].bitcast(I32), 0)
        load_scale_rows(nc.sync, w23_s, w2_scales, 0)
        load_scale_rows(nc.sync, w23_s, w3_scales, W3_SCALE_FIRST)
        s_ps = [psum.tile([P, S], F32, name="s_ps%d" % t, tag="bank%d" % (PLANES + t)) for t in range(PLANES)]

        tab_g = [tile("tab_g%d" % t, [P, S], F32) for t in range(PLANES)]
        factor = [tile("factor0", [P, PLANES, HALF], F32)]
        addend = [tile("addend0", [P, PLANES, HALF], F32)]
        for t in range(EARLY_TAB_PLANES):
            nc.scalar.activation(out=tab_g[t][:], in_=tab_early[:, t, :], func=ACT.Copy, scale=gk_sb[:, t : t + 1])
        for t in range(EARLY_TAB_PLANES):
            gather_on_scalar(factor[0][:, t, :], tab_g[t][:], entries(n3_l, 0, HALF))
            gather_on_scalar(addend[0][:, t, :], tab_g[t][:], entries(n4_l, 0, HALF))

        dt = []
        for t in range(PLANES):
            y_sb = tile("y_sb%d" % t, [P, S], F32)
            pa = tile_at("pa%d" % t, [P, PAIRS], F32, PLANE_BYTES * (t + 2))
            pb = tile_at("pb%d" % t, [P, PAIRS], F32, PLANE_BYTES * (t + 2) + PLANE_BYTES // 2)
            dt.append(tile_at("dt%d" % t, [P, S], F32, PLANE_BYTES * t))
            nc.scalar.copy(out=y_sb[:], in_=y_ps[t][:])
            gather_on_scalar(pa[:], y_sb[:], n1_l[:])
            gather_on_scalar(pb[:], y_sb[:], n2_l[:])
            nc.vector.tensor_tensor(out=dt[t][:].indirect(n1_l[:]), in0=pa[:], in1=pb[:], op=ALU.add)
            nc.vector.tensor_tensor(out=dt[t][:].indirect(n2_l[:]), in0=pa[:], in1=pb[:], op=ALU.mult)
            if t == 0:
                key_w_picked = tile_at("key_w_picked", [P, S], U32, PLANE_BYTES + PLANE_BYTES // 2)
                key_w = tile("key_w", [P, S], U32)
                nc.vector.tensor_copy(out=key_w_picked[:], in_=d_w[:].indirect(kidx_l[:]))
                nc.vector.tensor_copy(*deal_views(key_w[:].bitcast(I32), key_w_picked[:].bitcast(I32), LINE_WORDS))
                for u in range(PLANES):
                    product(s_ps[u][:], key_w, key_s, u, xt_w[:], xt_s[:], True, True)

        s_sb = [tile("s_sb%d" % t, [P, S], F32) for t in range(PLANES)]
        for t in range(PLANES):
            nc.scalar.activation(out=s_sb[t][:], in_=s_ps[t][:], func=ACT.Copy, scale=0.0625)
        for t in range(EARLY_TAB_PLANES, PLANES):
            nc.scalar.activation(
                out=tab_g[t][:], in_=tab_late[:, t - EARLY_TAB_PLANES, :], func=ACT.Copy, scale=gk_sb[:, t : t + 1]
            )

        w2_w = tile("w2_w", [P, S], U32, after="tab_early")
        w3_w = tile("w3_w", [P, S], U32, after="x_w")
        nc.sync.dma_start(out=w2_w[:].bitcast(I32), in_=words_view(w2_words))
        nc.sync.dma_start(out=w3_w[:].bitcast(I32), in_=words_view(w3_words))
        z2_w = tile("z2_w", [P, S], U32)
        z2_s = tile("z2_s", [P, S], U8)
        z_w = tile("z_w", [P, S], U32)
        z_s = tile("z_s", [P, S], U8)
        w2_w_dealt = tile("w2_w_dealt", [P, S], U32)
        w3_w_dealt = tile("w3_w_dealt", [P, S], U32)
        nc.scalar.copy(*deal_views(w2_w_dealt[:], w2_w[:], LINE_WORDS))
        nc.scalar.copy(*deal_views(w3_w_dealt[:], w3_w[:], LINE_WORDS))

        z_planes = tile("z_planes", [P, PLANES, S], BF16, after="key_w")
        for t in range(PLANES):
            gain = gn_sb[:, t : t + 1]
            if t < SCALAR_Z_PLANES:
                nc.scalar.activation(out=z_planes[:, t, :], in_=dt[t][:], func=ACT.Copy, scale=gain)
            else:
                nc.vector.tensor_scalar(out=z_planes[:, t, :], in0=dt[t][:], scalar1=gain, scalar2=None, op0=ALU.mult)
        z_woven = tile("z_woven", [P, PLANES * S], BF16)
        nc.vector.tensor_copy(out=woven_view(z_woven[:]), in_=planes_view(z_planes[:]))
        w23_s_dealt = tile("w23_s_dealt", [P, S], U8)
        nc.vector.tensor_copy(*deal_views(w23_s_dealt[:], w23_s[:], LINE_BYTES))
        nc.vector.quantize_mx(out=z_w[:].bitcast(FP8X4), scales=z_s[:], in_=z_woven[:])

        for half in range(2):
            start = HALF * half
            span = slice(start, start + HALF)
            picked_s = tile("picked_s%d" % half, [P, PLANES, HALF], F32)
            if half:
                factor.append(tile("factor1", [P, PLANES, HALF], F32, after="y_sb0"))
                addend.append(tile("addend1", [P, PLANES, HALF], F32, after="s_sb%d" % (PLANES - 1)))
            scaled = tile("scaled%d" % half, [P, PLANES, HALF], F32)
            z2_woven = tile("z2_woven%d" % half, [P, PLANES * HALF], BF16)
            tab_planes_left = range(0 if half else EARLY_TAB_PLANES, PLANES)
            for t in range(PLANES):
                gather_on_scalar(picked_s[:, t, :], s_sb[t][:], entries(n5_l, start, HALF))
            for t in tab_planes_left:
                gather_on_scalar(factor[half][:, t, :], tab_g[t][:], entries(n3_l, start, HALF))
            for t in tab_planes_left:
                gather_on_scalar(addend[half][:, t, :], tab_g[t][:], entries(n4_l, start, HALF))
            nc.vector.tensor_tensor(out=scaled[:], in0=picked_s[:], in1=factor[half][:], op=ALU.mult)
            nc.vector.tensor_tensor(
                out=woven_view(z2_woven[:]), in0=planes_view(scaled[:]), in1=planes_view(addend[half][:]), op=ALU.add
            )
            nc.vector.quantize_mx(out=z2_w[:, span].bitcast(FP8X4), scales=z2_s[:, span], in_=z2_woven[:])

        h = tile("h", [P, PLANES, S], F32)
        h_sq = tile("h_sq", [P, PLANES, S], F32)
        for half in range(2):
            span = slice(HALF * half, HALF * (half + 1))
            h_ps = [
                psum.tile([P, HALF], F32, name="h_ps%d_%d" % (half, t), tag="bank%d" % (PLANES * half + t))
                for t in range(PLANES)
            ]
            for t in range(PLANES):
                product(h_ps[t][:], w2_w_dealt, w23_s_dealt, t, z_w[:, span], z_s[:, span], True, False)
            for t in range(PLANES):
                product(h_ps[t][:], w3_w_dealt, w23_s_dealt[W3_SCALE_FIRST:P, :], t, z2_w[:, span], z2_s[:, span], False, True)
            for t in range(PLANES):
                if half:
                    nc.vector.tensor_copy(out=h[:, t, span], in_=h_ps[t][:])
                else:
                    nc.scalar.copy(out=h[:, t, span], in_=h_ps[t][:])
            if half == 0:
                nc.scalar.activation(out=h_sq[:, :, span], in_=h[:, :, span], func=ACT.Square)

        out_w = tile("out_w", [P, S], U32)
        out_s = tile("out_s", [P, S], U8)
        out_rows = out_0.rearrange("(p t) j -> p t j", t=PLANES)
        out_words = words_view(out_1)
        for piece, (start, width) in enumerate(OUT_PIECES):
            span = slice(start, start + width)
            shape = [P, PLANES, width]
            pa2 = tile("pa2_%d" % piece, shape, F32)
            pa2_sq = tile("pa2_sq%d" % piece, shape, F32)
            cross = tile("cross%d" % piece, shape, F32)
            squares = tile("squares%d" % piece, shape, F32)
            root = tile("root%d" % piece, shape, F32, after="root")
            inverse = tile("inverse%d" % piece, shape, F32)
            result = tile("result%d" % piece, shape, F32)
            out_woven = tile("out_woven%d" % piece, [P, PLANES * width], BF16)
            for t in range(PLANES):
                if t % 2:
                    gather_on_scalar(pa2[:, t, :], h[:, t, :], entries(n6_l, start, width))
                else:
                    nc.vector.tensor_copy(out=pa2[:, t, :], in_=h[:, t, :].indirect(entries(n6_l, start, width)))
            if start >= HALF:
                nc.scalar.activation(out=h_sq[:, :, span], in_=h[:, :, span], func=ACT.Square)
            nc.scalar.activation(out=pa2_sq[:], in_=pa2[:], func=ACT.Square)
            nc.vector.tensor_tensor(out=cross[:], in0=pa2[:], in1=h[:, :, span], op=ALU.mult)
            nc.vector.tensor_tensor(out=squares[:], in0=pa2_sq[:], in1=h_sq[:, :, span], op=ALU.add)
            nc.scalar.activation(out=root[:], in_=squares[:], func=ACT.Abs_reciprocal_sqrt, scale=0.5, bias=quarter[:])
            nc.scalar.activation(out=inverse[:], in_=root[:], func=ACT.Square)
            nc.vector.tensor_tensor(out=result[:], in0=cross[:], in1=inverse[:], op=ALU.mult)
            nc.sync.dma_start(out=out_rows[:, :, span], in_=result[:])
            nc.vector.tensor_copy(out=woven_view(out_woven[:]), in_=planes_view(result[:]))
            nc.vector.quantize_mx(out=out_w[:, span].bitcast(FP8X4), scales=out_s[:, span], in_=out_woven[:])
            nc.sync.dma_start(out=out_words[:, span], in_=out_w[:, span].bitcast(I32))
        for q in range(QUADRANTS):
            queue = nc.scalar if q % 2 else nc.sync
            queue.dma_start(
                out=out_2[0, 4 * q : 4 * q + 4, :].bitcast(I32), in_=out_s[32 * q : 32 * q + 4, :].bitcast(I32)
            )
